import numpy as np
import ml_dtypes


def mxq(x, axis, fmt="e4m3"):
    dtype, down = {"e4m3": (ml_dtypes.float8_e4m3fn, 7), "e5m2": (ml_dtypes.float8_e5m2, 14)}[fmt]
    v = np.moveaxis(np.asarray(x, np.float32).astype(ml_dtypes.bfloat16).astype(np.float64), axis, -1)
    blocks = v.reshape(v.shape[:-1] + (-1, 32))
    amax = np.abs(blocks).max(-1, keepdims=True)
    byte = np.maximum(np.where(amax > 0, np.frexp(amax)[1] - 1 + 127, 0) - down, 1)
    scale = np.exp2(byte - 127.0)
    codes = (blocks / scale).astype(np.float32).astype(dtype).astype(np.float64)
    return np.moveaxis((codes * scale).reshape(v.shape), -1, axis)


WIDE = False


def mx_kscale(k):
    if not WIDE:
        return np.ones(k)
    levels = np.array([10, -10, 5, -5, 0])
    if k % 512:
        return np.exp2(np.random.permutation(np.resize(levels, k // 32))).repeat(32)
    a = np.empty((k // 512, 16))
    for p in range(k // 512):
        a[p, :8] = np.random.permutation(np.resize(levels, 8))
        for g in range(8):
            far = levels[np.abs(levels - a[p, g]) >= 10]
            a[p, g + 8] = far[np.random.randint(len(far))]
    return np.exp2(a.ravel()).repeat(32)


def f64(x):
    return np.asarray(x).astype(np.float64)


def striped(idx):
    return np.tile(idx.reshape(-1, 16).T, (8, 1)).astype(np.uint16)


def unstriped(offs):
    return offs[:16].T.reshape(-1).astype(np.int64)


E2M1 = np.array([0.0, 0.5, 1.0, 1.5, 2.0, 3.0, 4.0, 6.0, -0.0, -0.5, -1.0, -1.5, -2.0, -3.0, -4.0, -6.0])


def pack_weight(w, fmt):
    k, n = w.shape
    w = f64(np.asarray(w, np.float32).astype(ml_dtypes.bfloat16)).reshape(k // 32, 32, n)
    amax = np.abs(w).max(1)
    if fmt == "e4m3":
        byte = np.frexp(amax)[1] - 1 + 127 - 7
    else:
        mant, ex = np.frexp(amax / 6.0)
        byte = np.where(mant > 0.5, ex, ex - 1) + 127
    byte = np.clip(np.where(amax > 0, byte, 1), 1, 254)
    scaled = (w * np.exp2(127.0 - byte)[:, None, :]).reshape(k, n).astype(np.float32)
    by_word = np.ascontiguousarray(scaled.reshape(k // 512, 128, 4, n).transpose(0, 1, 3, 2))
    if fmt == "e4m3":
        words = by_word.astype(ml_dtypes.float8_e4m3fn).view(np.uint8)
    else:
        c = by_word.astype(ml_dtypes.float4_e2m1fn).view(np.uint8) & 0xF
        words = (c[..., 0::2] | (c[..., 1::2] << 4)).reshape(k // 512, 128, 2 * n)
    return np.ascontiguousarray(words), np.ascontiguousarray(byte.astype(np.uint8).reshape(k // 512, 16, n))


def unpack_weight(words, scales, fmt):
    g, _, n = scales.shape
    words = np.ascontiguousarray(words).reshape(g, 128, n, -1)
    if fmt == "e4m3":
        vals = words.view(ml_dtypes.float8_e4m3fn).astype(np.float64)
    else:
        nib = np.empty((g, 128, n, 4), np.uint8)
        nib[..., 0::2] = words & 0xF
        nib[..., 1::2] = words >> 4
        vals = E2M1[nib]
    vals = vals * np.repeat(np.exp2(scales.astype(np.float64) - 127.0), 8, axis=1)[..., None]
    return vals.transpose(0, 1, 3, 2).reshape(g * 512, n)


def planes(y):
    n, m = y.shape
    v = y.astype(np.float32).astype(ml_dtypes.bfloat16).astype(np.float64).reshape(n // 32, 32, m)
    top = np.abs(v).max(1)
    byte = np.clip(np.where(top > 0, np.frexp(top)[1] - 1 + 127 - 7, 1), 1, 254)
    codes = (v * np.exp2(127.0 - byte)[:, None, :]).reshape(n, m).astype(np.float32).astype(ml_dtypes.float8_e4m3fn).view(np.uint8)
    words = codes.reshape(n // 512, 128, 4, m).transpose(0, 1, 3, 2)
    return np.ascontiguousarray(words), np.ascontiguousarray(byte.astype(np.uint8).reshape(n // 512, 16, m))


def silu(v):
    return v / (1.0 + np.exp(-np.maximum(v, -700.0)))


K, T, E, C, H, N, HOT = 1024, 768, 6, 256, 512, 512, 3


def by_expert(wq, xq):
    return np.concatenate([wq[e].T @ xq[:, e * C:(e + 1) * C] for e in range(E)], axis=1)


def setup_inputs():
    n = np.random.standard_normal
    s = mx_kscale(K)
    u = mx_kscale(H)
    slot_token = np.concatenate([np.random.permutation(T)[:C] for e in range(E)])
    x = pack_weight(n((K, T)) * s[:, None], "e4m3")
    w1h = [pack_weight(m, "e4m3") for m in n((HOT, K, H)) / np.sqrt(K) / s[None, :, None] * u]
    w2h = [pack_weight(m, "e4m3") for m in n((HOT, H, N)) / np.sqrt(H) / u[None, :, None]]
    w1c = [pack_weight(m, "e2m1") for m in n((E - HOT, K, H)) / np.sqrt(K) / s[None, :, None] * u]
    w2c = [pack_weight(m, "e2m1") for m in n((E - HOT, H, N)) / np.sqrt(H) / u[None, :, None]]
    return {
        "x_words": x[0],
        "x_scales": x[1],
        "w1h_words": np.stack([m[0] for m in w1h]),
        "w1h_scales": np.stack([m[1] for m in w1h]),
        "w2h_words": np.stack([m[0] for m in w2h]),
        "w2h_scales": np.stack([m[1] for m in w2h]),
        "w1c_words": np.stack([m[0] for m in w1c]),
        "w1c_scales": np.stack([m[1] for m in w1c]),
        "w2c_words": np.stack([m[0] for m in w2c]),
        "w2c_scales": np.stack([m[1] for m in w2c]),
        "offs": striped(slot_token),
    }


def reference(x_words, x_scales, w1h_words, w1h_scales, w2h_words, w2h_scales, w1c_words, w1c_scales, w2c_words, w2c_scales, offs):
    w1h = np.stack([unpack_weight(w1h_words[e], w1h_scales[e], "e4m3") for e in range(HOT)])
    w2h = np.stack([unpack_weight(w2h_words[e], w2h_scales[e], "e4m3") for e in range(HOT)])
    w1c = np.stack([unpack_weight(w1c_words[e], w1c_scales[e], "e2m1") for e in range(E - HOT)])
    w2c = np.stack([unpack_weight(w2c_words[e], w2c_scales[e], "e2m1") for e in range(E - HOT)])
    idx = unstriped(offs)
    xq = unpack_weight(x_words, x_scales, "e4m3")[:, idx]
    w1 = [*w1h, *w1c]
    w2 = [*w2h, *w2c]
    h = silu(by_expert(w1, xq))
    y = by_expert(w2, mxq(h, 0, "e4m3"))
    out = y
    out_0 = out
    return (out_0,) + planes(out_0)

@@ -1,0 +1,309 @@
+from contextlib import ExitStack
+
+import concourse.mybir as mybir
+from concourse.masks import make_identity
+
+K, T, E, C, H, N, HOT = 1024, 768, 6, 256, 512, 512, 3
+COLD = E - HOT
+SLOTS = E * C
+FLOPS = 2 * SLOTS * (K * H + H * N)
+
+F32 = mybir.dt.float32
+BF16 = mybir.dt.bfloat16
+I32 = mybir.dt.int32
+U32 = mybir.dt.uint32
+U16 = mybir.dt.uint16
+U8 = mybir.dt.uint8
+FP8X4 = mybir.dt.float8_e4m3fn_x4
+FP4X4 = mybir.dt.float4_e2m1fn_x4
+SILU = mybir.ActivationFunctionType.Silu
+
+P = 128
+PASSES = K // 512
+BLK = 128
+PER_COL = 16
+W1H_ROW = 4
+W2H_ROW = 8
+SCALAR_ROUNDS = ()
+VECTOR_TURNED = (3,4,5)
+VECTOR_EMPTIES = ()
+LOADS = "x0 x1 xs a0 hay a1 a2 cag cbg a3 hby b0 b1 a4 b2 a5 b3"
+FIRST = 2
+GATE = "x"
+REST_CUTS = ((768, 384), (1152, 384), (512, 256))
+XG_BUFS = (2,2)
+BANKS = (3,2,3)
+SHIFT = "g"
+CODE_STORES = (512,1024,1408,1536)
+SCALE_STORES = "sysy"
+STEPS = "s0 s1 g0 g1 A0 s2 g2 A1 A2 d0 g3 B0 g4 A3 A4 r0 d1 B1 g5 p0 d2 A5 B2 r1 p1 d4 r2 d3 B3 p2 r3 B4 p3 d5 r4 B5 p4"
+
+
+def load_scale_rows(queue, plane, row0, rows):
+    planes = rows.shape[0]
+    by_r = rows.rearrange("g (q r) j -> r q g j", r=4)
+    for r in range(4):
+        dst = plane[row0 + r : P : 32, :].bitcast(I32).rearrange("q (g j) -> q g j", g=planes)
+        queue.dma_start(out=dst, in_=by_r[r].bitcast(I32))
+
+
+def tile_moe_hot_s_mlp_silu_kernel(
+    tc, x_words, x_scales, w1h_words, w1h_scales, w2h_words, w2h_scales,
+    w1c_words, w1c_scales, w2c_words, w2c_scales, offs, out_0, out_1, out_2,
+):
+    nc = tc.nc
+    with ExitStack() as ctx:
+        keep = ctx.enter_context(tc.tile_pool(name="keep", bufs=1))
+        ring = ctx.enter_context(tc.tile_pool(name="ring", bufs=4))
+        psum = ctx.enter_context(tc.psum_pool(name="psum", bufs=1))
+
+        def held(shape, dtype, name):
+            return keep.tile(shape, dtype, name=name, align_bytes=64)
+
+        offsets = keep.tile([P, SLOTS // PER_COL], U16, name="offsets")
+        xs = held([P, T], U8, "xs")
+        w1hs = held([P, HOT * PASSES * H], U8, "w1hs")
+        w1cs = held([P, COLD * PASSES * H], U8, "w1cs")
+        w2s_raw = held([P, HOT * N], U8, "w2s_raw")
+        sg_cold1 = held([P, COLD * C], U8, "sg_cold1")
+        ident = held([P, P], F32, "ident")
+
+        for plane in (xs, w1hs, w2s_raw, w1cs, sg_cold1):
+            nc.vector.memset(plane[:].bitcast(I32), 0)
+        make_identity(nc, ident[:])
+
+        nc.sync.dma_start(offsets[:], offs)
+        xw = [held([P, T], I32, "xw%d" % s) for s in range(PASSES)]
+
+        def load_x(s):
+            nc.sync.dma_start(out=xw[s][:], in_=x_words[s].rearrange("p t d -> p (t d)").bitcast(I32))
+
+        def load_xs():
+            for q in range(4):
+                nc.sync.dma_start(out=xs[32 * q : 32 * q + 8, :].bitcast(I32), in_=x_scales[:, 4 * q : 4 * q + 4, :].bitcast(I32))
+
+        w1 = [None] * E
+        w2_raw = [None] * E
+
+        def load_w1(e):
+            if e < HOT:
+                w1[e] = held([P, PASSES, H], I32, "w1h%d" % e)
+                nc.sync.dma_start(out=w1[e][:], in_=w1h_words[e].rearrange("s p i d -> p s (i d)").bitcast(I32))
+            else:
+                w1[e] = held([P, PASSES, H // 2], I32, "w1c%d" % e)
+                nc.sync.dma_start(out=w1[e][:], in_=w1c_words[e - HOT].rearrange("s p b -> p s b").bitcast(I32))
+
+        def load_w2(e):
+            if e < HOT:
+                w2_raw[e] = held([P, N], I32, "w2h_raw%d" % e)
+                nc.sync.dma_start(out=w2_raw[e][:], in_=w2h_words[e, 0].rearrange("p n d -> p (n d)").bitcast(I32))
+            else:
+                w2_raw[e] = held([P, COLD * N // 2], I32, "w2c_raw")
+                nc.sync.dma_start(
+                    out=w2_raw[e][:].rearrange("p (f b) -> p f b", f=COLD),
+                    in_=w2c_words.rearrange("f s p b -> p (f s) b").bitcast(I32),
+                )
+
+        queues = {"y": nc.sync, "s": nc.scalar, "g": nc.gpsimd}
+        for item in LOADS.split():
+            if item == "xs":
+                load_xs()
+            elif item.startswith("x"):
+                load_x(int(item[1]))
+            elif item.startswith("a"):
+                load_w1(int(item[1]))
+            elif item.startswith("b"):
+                load_w2(int(item[1]))
+            elif item.startswith("ha"):
+                load_scale_rows(queues[item[2]], w1hs, W1H_ROW, w1h_scales.rearrange("e s b i -> (e s) b i"))
+            elif item.startswith("ca"):
+                load_scale_rows(queues[item[2]], w1cs, 0, w1c_scales.rearrange("e s b i -> (e s) b i"))
+            elif item.startswith("hb"):
+                load_scale_rows(queues[item[2]], w2s_raw, W2H_ROW, w2h_scales.rearrange("e s b n -> (e s) b n"))
+            else:
+                load_scale_rows(queues[item[2]], w2s_raw, 0, w2c_scales.rearrange("e s b n -> (e s) b n"))
+
+        def slot_list(first, count):
+            return offsets[:, first // PER_COL : (first + count) // PER_COL]
+
+        sg_own = [keep.tile([P, C], U8, name="sg_own%d" % e, tag="sg%d" % e, align_bytes=64) for e in range(FIRST)]
+        sg_rest = keep.tile([P, (E - FIRST) * C], U8, name="sg_rest", tag="sg%s" % GATE, align_bytes=64)
+        xg = [[None] * PASSES for e in range(E)]
+
+        def gather_words(e):
+            for s in range(PASSES):
+                xg[e][s] = ring.tile([P, C], U32, name="xg%d" % s, bufs=XG_BUFS[s], align_bytes=64)
+                nc.vector.tensor_copy(xg[e][s][:], xw[s][:].bitcast(U32).indirect(slot_list(e * C, C)))
+
+        def gather_scales(dst, first):
+            nc.vector.tensor_copy(dst, xs[:].indirect(slot_list(first, dst.shape[1])))
+
+        def token_scales(e, s, j):
+            if e < FIRST:
+                return sg_own[e][4 * s : P, j * BLK : (j + 1) * BLK]
+            if e < HOT or s == 0:
+                return sg_rest[4 * s : P, (e - FIRST) * C + j * BLK : (e - FIRST) * C + (j + 1) * BLK]
+            first = (e - HOT) * C + j * BLK
+            return sg_cold1[:, first : first + BLK]
+
+        hq = [held([P, 4 * C], BF16, "hq%d" % e) for e in range(E)]
+
+        def layer1(e):
+            turned = psum.tile([P, 2, 2, BLK], F32, name="turned", bufs=BANKS[1])
+            for j in range(C // BLK):
+                acc = psum.tile([P, H], F32, name="acc1", bufs=BANKS[0])
+                for s in range(PASSES):
+                    if e < HOT:
+                        g = e * PASSES + s
+                        rhs, rhs_scale = w1[e][:, s, :].bitcast(FP8X4), w1hs[W1H_ROW:P, g * H : (g + 1) * H]
+                    else:
+                        g = (e - HOT) * PASSES + s
+                        rhs, rhs_scale = w1[e][:, s, :].bitcast(FP4X4), w1cs[:, g * H : (g + 1) * H]
+                    nc.tensor.matmul_mx(
+                        out=acc[:], lhsT=xg[e][s][:, j * BLK : (j + 1) * BLK].bitcast(FP8X4), lhsT_scale=token_scales(e, s, j),
+                        rhs=rhs, rhs_scale=rhs_scale, start=(s == 0), stop=(s == PASSES - 1),
+                    )
+                hs = ring.tile([P, H], BF16, name="hs", align_bytes=64)
+                nc.scalar.activation(
+                    hs[:].rearrange("p (u q v) -> p u q v", u=2, v=2), acc[:].rearrange("p (q u v) -> p u q v", u=2, v=2), SILU,
+                )
+                words = hs[:].bitcast(F32)
+                for u in range(2):
+                    nc.tensor.transpose(turned[:, j, u, :], words[:, u * P : (u + 1) * P], ident[:])
+            empty = nc.vector.tensor_copy if e in VECTOR_TURNED else nc.scalar.copy
+            empty(hq[e][:].bitcast(F32).rearrange("p (j s u) -> p j s u", j=2, u=2), turned[:].rearrange("p j u s -> p j s u"))
+
+        w2s = [held([P, N], U8, "w2s%d" % f) for f in range(HOT)]
+        y_scales = held([P, SLOTS], U8, "y_scales")
+        y_rows = out_0.rearrange("(p t) j -> p t j", t=4)
+        word_rows = out_1[0].rearrange("p j d -> p (j d)").bitcast(I32)
+        w2 = [None] * E
+        y = [None] * E
+        yq = [None] * E
+
+        def deal(dst, src):
+            nc.vector.tensor_copy(dst.rearrange("p (t m) -> p m t", t=4), src.rearrange("p (m t) -> p m t", t=4))
+
+        def deal_w2(e):
+            if e < HOT:
+                w2[e] = held([P, N], I32, "w2h%d" % e)
+                deal(w2[e][:], w2_raw[e][:])
+                deal(w2s[e][:], w2s_raw[:, e * N : (e + 1) * N])
+            else:
+                f = e - HOT
+                w2[e] = held([P, N // 2], I32, "w2c%d" % f)
+                deal(w2[e][:].bitcast(U16), w2_raw[HOT][:, f * N // 2 : (f + 1) * N // 2].bitcast(U16))
+
+        def second_product(e, t, out, codes, scales):
+            if e < HOT:
+                lhsT = w2[e][:, t * P : (t + 1) * P].bitcast(FP8X4)
+                lhsT_scale = w2s[e][W2H_ROW:P, t * P : (t + 1) * P]
+            else:
+                lhsT = w2[e][:, t * P // 2 : (t + 1) * P // 2].bitcast(FP4X4)
+                lhsT_scale = w2s[e - HOT][:, t * P : (t + 1) * P]
+            nc.tensor.matmul_mx(
+                out=out, lhsT=lhsT, lhsT_scale=lhsT_scale, rhs=codes.bitcast(FP8X4), rhs_scale=scales, start=True, stop=True,
+            )
+
+        last = []
+
+        def layer2(e):
+            h_codes = held([P, C], U32, "h_codes%d" % e)
+            h_scales = held([P, C], U8, "h_scales%d" % e)
+            nc.vector.quantize_mx(out=h_codes[:].bitcast(FP8X4), scales=h_scales[:], in_=hq[e][:])
+            if e == E - 1:
+                for j in range(C // BLK):
+                    cols = slice(j * BLK, (j + 1) * BLK)
+                    slots = slice(e * C + j * BLK, e * C + (j + 1) * BLK)
+                    acc = psum.tile([P, 4 * BLK], F32, name="acc2", bufs=BANKS[2])
+                    quarters = acc[:].rearrange("p (t s) -> p t s", t=4)
+                    for t in range(4):
+                        second_product(e, t, quarters[:, t, :], h_codes[:, cols], h_scales[:, cols])
+                    half_q = held([P, 4 * BLK], BF16, "yq_last%d" % j)
+                    half = held([P, 4, BLK], F32, "y_last%d" % j)
+                    if j == 0:
+                        nc.vector.tensor_copy(half_q[:].rearrange("p (s t) -> p s t", t=4), quarters.rearrange("p t s -> p s t"))
+                    nc.scalar.copy(half[:], quarters)
+                    if j == 1:
+                        nc.vector.tensor_copy(half_q[:].rearrange("p (s t) -> p s t", t=4), quarters.rearrange("p t s -> p s t"))
+                    nc.sync.dma_start(out=y_rows[:, :, slots], in_=half[:])
+                    last.append((half_q, slots))
+                return
+            y[e] = held([P, 4, C], F32, "y%d" % e)
+            yq[e] = held([P, 4 * C], BF16, "yq%d" % e)
+            if e in SCALAR_ROUNDS:
+                for j in range(C // BLK):
+                    cols = slice(j * BLK, (j + 1) * BLK)
+                    acc = psum.tile([P, 4 * BLK], F32, name="acc2", bufs=BANKS[2])
+                    quarters = acc[:].rearrange("p (t s) -> p t s", t=4)
+                    for t in range(4):
+                        second_product(e, t, quarters[:, t, :], h_codes[:, cols], h_scales[:, cols])
+                    nc.scalar.copy(y[e][:, :, cols], quarters)
+                    nc.scalar.copy(
+                        yq[e][:, 4 * j * BLK : 4 * (j + 1) * BLK].rearrange("p (s t) -> p s t", t=4), quarters.rearrange("p t s -> p s t"),
+                    )
+            else:
+                for pair in range(2):
+                    acc = psum.tile([P, 2 * C], F32, name="acc2", bufs=BANKS[2])
+                    for v in range(2):
+                        second_product(e, 2 * pair + v, acc[:, v * C : (v + 1) * C], h_codes[:], h_scales[:])
+                    empty = nc.vector.tensor_copy if (e, pair) in VECTOR_EMPTIES else nc.scalar.copy
+                    empty(y[e][:, 2 * pair : 2 * pair + 2, :], acc[:].rearrange("p (v s) -> p v s", v=2))
+            nc.sync.dma_start(out=y_rows[:, :, e * C : (e + 1) * C], in_=y[e][:])
+
+        def round_y(e):
+            if e not in SCALAR_ROUNDS:
+                nc.vector.tensor_copy(
+                    yq[e][:].rearrange("p (c i t) -> p c t i", i=4, t=4), y[e][:].rearrange("p t (c i) -> p c t i", i=4),
+                )
+
+        y_codes = held([P, SLOTS], I32, "y_codes")
+
+        def planes(source, slots):
+            nc.vector.quantize_mx(out=y_codes[:, slots].bitcast(FP8X4), scales=y_scales[:, slots], in_=source[:])
+            if slots.stop in CODE_STORES:
+                first = max([0] + [c for c in CODE_STORES if c < slots.stop])
+                nc.sync.dma_start(out=word_rows[:, first : slots.stop], in_=y_codes[:, first : slots.stop])
+
+        def rest_scales():
+            for first, width in REST_CUTS:
+                gather_scales(sg_rest[:, first - FIRST * C : first - FIRST * C + width], first)
+            cold0 = sg_rest[:, (HOT - FIRST) * C : (E - FIRST) * C]
+            if SHIFT == "g":
+                nc.gpsimd.dma_start(out=sg_cold1[0 : P - 4, :].bitcast(I32), in_=cold0[4:P, :].bitcast(I32))
+            else:
+                for r in range(4):
+                    queues[SHIFT].dma_start(out=sg_cold1[r:P:32, :].bitcast(I32), in_=cold0[4 + r : P : 32, :].bitcast(I32))
+
+        for item in STEPS.split():
+            e = int(item[1])
+            if item[0] == "s":
+                if e < FIRST:
+                    gather_scales(sg_own[e][:], e * C)
+                else:
+                    rest_scales()
+            elif item[0] == "w":
+                idle = psum.tile([P, H], F32, name="acc2", bufs=BANKS[2])
+                for n in range(e):
+                    nc.tensor.matmul_mx(
+                        out=idle[:, (n % 2) * C : (n % 2 + 1) * C], lhsT=xg[0][0][:, 0:BLK].bitcast(FP8X4), lhsT_scale=sg_own[0][:, 0:BLK],
+                        rhs=xg[0][0][:].bitcast(FP8X4), rhs_scale=sg_own[0][:], start=True, stop=True,
+                    )
+            elif item[0] == "g":
+                gather_words(e)
+            elif item[0] == "A":
+                layer1(e)
+            elif item[0] == "d":
+                deal_w2(e)
+            elif item[0] == "B":
+                layer2(e)
+            elif item[0] == "r":
+                round_y(e)
+            else:
+                planes(yq[e], slice(e * C, (e + 1) * C))
+        for source, slots in last:
+            planes(source, slots)
+        for q in range(4):
+            queues[SCALE_STORES[q]].dma_start(
+                out=out_2[0, 4 * q : 4 * q + 4, :].bitcast(I32), in_=y_scales[32 * q : 32 * q + 4, :].bitcast(I32),
+            )

@@ -25,18 +25,20 @@ PER_COL = 16
 W1H_ROW = 4
 W2H_ROW = 8
 SCALAR_ROUNDS = ()
-VECTOR_TURNED = (3,4,5)
-VECTOR_EMPTIES = ()
-LOADS = "x0 x1 xs a0 hay a1 a2 cag cbg a3 hby b0 b1 a4 b2 a5 b3"
+VECTOR_TURNED = ()
+VECTOR_EMPTIES = ((2,0),)
+LOADS = "x0 x1 xs a0 hay a1 a2 cay C b0 hby cbg b1 b2 b3"
 FIRST = 2
 GATE = "x"
-REST_CUTS = ((768, 384), (1152, 384), (512, 256))
+REST_CUTS = ((512, 256), (768, 384), (1152, 384))
 XG_BUFS = (2,2)
 BANKS = (3,2,3)
 SHIFT = "g"
-CODE_STORES = (512,1024,1408,1536)
-SCALE_STORES = "sysy"
-STEPS = "s0 s1 g0 g1 A0 s2 g2 A1 A2 d0 g3 B0 g4 A3 A4 r0 d1 B1 g5 p0 d2 A5 B2 r1 p1 d4 r2 d3 B3 p2 r3 B4 p3 d5 r4 B5 p4"
+CODE_STORES = (768,1280,1536)
+SCALE_STORES = "ssyy"
+STEPS = "s0 g0 g1 e0 e1 g2 d0 A0 g3 s1 B0 d2 g4 s2 A1 A2 r0 d1 B1 d4 r1 g5 e2 d3 A3 p0 A4 B2 A5 B3 r2 B4 r3 d5 p1 p2 r4 p3 B5 p4"
+LAST = "svsv"
+REUSE = {5: 2}
 
 
 def load_scale_rows(queue, plane, row0, rows):
@@ -87,7 +89,7 @@ def tile_moe_hot_s_mlp_silu_kernel(
 
         def load_w1(e):
             if e < HOT:
-                w1[e] = held([P, PASSES, H], I32, "w1h%d" % e)
+                w1[e] = keep.tile([P, PASSES, H], I32, name="w1h%d" % e, tag="w1h%d" % e, align_bytes=64)
                 nc.sync.dma_start(out=w1[e][:], in_=w1h_words[e].rearrange("s p i d -> p s (i d)").bitcast(I32))
             else:
                 w1[e] = held([P, PASSES, H // 2], I32, "w1c%d" % e)
@@ -110,6 +112,18 @@ def tile_moe_hot_s_mlp_silu_kernel(
                 load_xs()
             elif item.startswith("x"):
                 load_x(int(item[1]))
+            elif item == "C":
+                cold = held([P, COLD * PASSES, H // 2], I32, "w1c")
+                nc.sync.dma_start(out=cold[:], in_=w1c_words.rearrange("f s p b -> p (f s) b").bitcast(I32))
+                for f in range(COLD):
+                    w1[HOT + f] = cold[:, f * PASSES : (f + 1) * PASSES, :]
+            elif item == "B":
+                hot = held([P, HOT * N], I32, "w2h_raw")
+                nc.sync.dma_start(
+                    out=hot[:].rearrange("p (e w) -> p e w", e=HOT), in_=w2h_words.rearrange("e s p n d -> p (e s) (n d)").bitcast(I32),
+                )
+                for e in range(HOT):
+                    w2_raw[e] = hot[:, e * N : (e + 1) * N]
             elif item.startswith("a"):
                 load_w1(int(item[1]))
             elif item.startswith("b"):
@@ -131,8 +145,13 @@ def tile_moe_hot_s_mlp_silu_kernel(
         xg = [[None] * PASSES for e in range(E)]
 
         def gather_words(e):
+            if e in REUSE:
+                both = keep.tile([P, PASSES * C], U32, name="xg_both%d" % e, tag="w1h%d" % REUSE[e], align_bytes=64)
             for s in range(PASSES):
-                xg[e][s] = ring.tile([P, C], U32, name="xg%d" % s, bufs=XG_BUFS[s], align_bytes=64)
+                if e in REUSE:
+                    xg[e][s] = both[:, s * C : (s + 1) * C]
+                else:
+                    xg[e][s] = ring.tile([P, C], U32, name="xg%d" % s, bufs=XG_BUFS[s], align_bytes=64)
                 nc.vector.tensor_copy(xg[e][s][:], xw[s][:].bitcast(U32).indirect(slot_list(e * C, C)))
 
         def gather_scales(dst, first):
@@ -181,18 +200,20 @@ def tile_moe_hot_s_mlp_silu_kernel(
         y = [None] * E
         yq = [None] * E
 
-        def deal(dst, src):
-            nc.vector.tensor_copy(dst.rearrange("p (t m) -> p m t", t=4), src.rearrange("p (m t) -> p m t", t=4))
+        def deal(dst, src, width):
+            line = 16 * dst.shape[1] // width
+            nc.vector.tensor_copy(
+                dst.rearrange("p (t b i) -> p b t i", t=4, i=line), src.rearrange("p (b i t) -> p b t i", t=4, i=line),
+            )
 
         def deal_w2(e):
             if e < HOT:
                 w2[e] = held([P, N], I32, "w2h%d" % e)
-                deal(w2[e][:], w2_raw[e][:])
-                deal(w2s[e][:], w2s_raw[:, e * N : (e + 1) * N])
+                deal(w2[e][:], w2_raw[e][:], 4 * N)
             else:
                 f = e - HOT
                 w2[e] = held([P, N // 2], I32, "w2c%d" % f)
-                deal(w2[e][:].bitcast(U16), w2_raw[HOT][:, f * N // 2 : (f + 1) * N // 2].bitcast(U16))
+                deal(w2[e][:].bitcast(U16), w2_raw[HOT][:, f * N // 2 : (f + 1) * N // 2].bitcast(U16), 2 * N)
 
         def second_product(e, t, out, codes, scales):
             if e < HOT:
@@ -221,11 +242,9 @@ def tile_moe_hot_s_mlp_silu_kernel(
                         second_product(e, t, quarters[:, t, :], h_codes[:, cols], h_scales[:, cols])
                     half_q = held([P, 4 * BLK], BF16, "yq_last%d" % j)
                     half = held([P, 4, BLK], F32, "y_last%d" % j)
-                    if j == 0:
-                        nc.vector.tensor_copy(half_q[:].rearrange("p (s t) -> p s t", t=4), quarters.rearrange("p t s -> p s t"))
-                    nc.scalar.copy(half[:], quarters)
-                    if j == 1:
-                        nc.vector.tensor_copy(half_q[:].rearrange("p (s t) -> p s t", t=4), quarters.rearrange("p t s -> p s t"))
+                    copies = {"v": nc.vector.tensor_copy, "s": nc.scalar.copy}
+                    copies[LAST[2 * j]](half_q[:].rearrange("p (s t) -> p s t", t=4), quarters.rearrange("p t s -> p s t"))
+                    copies[LAST[2 * j + 1]](half[:], quarters)
                     nc.sync.dma_start(out=y_rows[:, :, slots], in_=half[:])
                     last.append((half_q, slots))
                 return
@@ -293,6 +312,8 @@ def tile_moe_hot_s_mlp_silu_kernel(
                 gather_words(e)
             elif item[0] == "A":
                 layer1(e)
+            elif item[0] == "e":
+                deal(w2s[e][:], w2s_raw[:, e * N : (e + 1) * N], N)
             elif item[0] == "d":
                 deal_w2(e)
             elif item[0] == "B":

@@ -25,20 +25,26 @@ PER_COL = 16
 W1H_ROW = 4
 W2H_ROW = 8
 SCALAR_ROUNDS = ()
-VECTOR_TURNED = ()
-VECTOR_EMPTIES = ((2,0),)
-LOADS = "x0 x1 xs a0 hay a1 a2 cay C b0 hby cbg b1 b2 b3"
+VECTOR_TURNED = (3,4)
+VECTOR_EMPTIES = ()
+LOADS = "x0 x1 xs a0 hay a1 a2 cag a3 b0 hby | cbg b1 a4 a5 b2 b3"
 FIRST = 2
 GATE = "x"
-REST_CUTS = ((512, 256), (768, 384), (1152, 384))
+REST_CUTS = ((1024, 512), (512, 512))
 XG_BUFS = (2,2)
-BANKS = (3,2,3)
-SHIFT = "g"
-CODE_STORES = (768,1280,1536)
-SCALE_STORES = "ssyy"
-STEPS = "s0 g0 g1 e0 e1 g2 d0 A0 g3 s1 B0 d2 g4 s2 A1 A2 r0 d1 B1 d4 r1 g5 e2 d3 A3 p0 A4 B2 A5 B3 r2 B4 r3 d5 p1 p2 r4 p3 B5 p4"
-LAST = "svsv"
-REUSE = {5: 2}
+BANKS = (3,1,4)
+SHIFT = "y"
+CODE_STORES = (256,768,1280,1536)
+SCALE_STORES = "ssss"
+STEPS = "g0 s0 g1 g2 s1 g3 s2 A0 d0 d4 d1 g4 d3 e1 d2 e0 e2 B0 A1 A2 B1 A3 r0 r1 p0 g5 p1 A4 B2 B3 r2 B4 A5 d5 r4 r3 p2 p3 p4 B5"
+LAST = "n"
+REUSE = {}
+Y_GROUPS = ((0,),(1,),(2,),(3,),(4,))
+LAST_WHOLE = False
+Y_FIRST = True
+BANK_STORES = (3,4,5)
+SCALE_SPLIT = 0
+XS_QUEUES = "ggyy"
 
 
 def load_scale_rows(queue, plane, row0, rows):
@@ -64,15 +70,20 @@ def tile_moe_hot_s_mlp_silu_kernel(
 
         offsets = keep.tile([P, SLOTS // PER_COL], U16, name="offsets")
         xs = held([P, T], U8, "xs")
-        w1hs = held([P, HOT * PASSES * H], U8, "w1hs")
+        if "hp" in LOADS:
+            w1hs = held([P, H], U8, "w1hs")
+            w1hs2 = held([P, H], U8, "w1hs2")
+            late_planes = (w1hs2,)
+        else:
+            w1hs = held([P, HOT * PASSES * H], U8, "w1hs")
+            late_planes = ()
         w1cs = held([P, COLD * PASSES * H], U8, "w1cs")
         w2s_raw = held([P, HOT * N], U8, "w2s_raw")
         sg_cold1 = held([P, COLD * C], U8, "sg_cold1")
         ident = held([P, P], F32, "ident")
 
-        for plane in (xs, w1hs, w2s_raw, w1cs, sg_cold1):
+        for plane in (xs, w1hs, w2s_raw, w1cs, sg_cold1) + late_planes:
             nc.vector.memset(plane[:].bitcast(I32), 0)
-        make_identity(nc, ident[:])
 
         nc.sync.dma_start(offsets[:], offs)
         xw = [held([P, T], I32, "xw%d" % s) for s in range(PASSES)]
@@ -82,7 +93,10 @@ def tile_moe_hot_s_mlp_silu_kernel(
 
         def load_xs():
             for q in range(4):
-                nc.sync.dma_start(out=xs[32 * q : 32 * q + 8, :].bitcast(I32), in_=x_scales[:, 4 * q : 4 * q + 4, :].bitcast(I32))
+                queues[XS_QUEUES[q]].dma_start(
+                    out=xs[32 * q : 32 * q + 8, :].bitcast(I32), in_=x_scales[:, 4 * q : 4 * q + 4, :].bitcast(I32),
+                )
+            make_identity(nc, ident[:])
 
         w1 = [None] * E
         w2_raw = [None] * E
@@ -107,7 +121,7 @@ def tile_moe_hot_s_mlp_silu_kernel(
                 )
 
         queues = {"y": nc.sync, "s": nc.scalar, "g": nc.gpsimd}
-        for item in LOADS.split():
+        def load(item):
             if item == "xs":
                 load_xs()
             elif item.startswith("x"):
@@ -128,6 +142,13 @@ def tile_moe_hot_s_mlp_silu_kernel(
                 load_w1(int(item[1]))
             elif item.startswith("b"):
                 load_w2(int(item[1]))
+            elif item.startswith("hp") or item.startswith("hq"):
+                rows = w1h_scales.rearrange("e s b i -> (e s) b i")
+                plane, rows = (w1hs, rows[0:4]) if item[1] == "p" else (w1hs2, rows[4:6])
+                for q in range(4):
+                    queues[item[2]].dma_start(
+                        out=plane[32 * q : 32 * q + 4 * rows.shape[0], :].bitcast(I32), in_=rows[:, 4 * q : 4 * q + 4, :].bitcast(I32),
+                    )
             elif item.startswith("ha"):
                 load_scale_rows(queues[item[2]], w1hs, W1H_ROW, w1h_scales.rearrange("e s b i -> (e s) b i"))
             elif item.startswith("ca"):
@@ -136,6 +157,9 @@ def tile_moe_hot_s_mlp_silu_kernel(
                 load_scale_rows(queues[item[2]], w2s_raw, W2H_ROW, w2h_scales.rearrange("e s b n -> (e s) b n"))
             else:
                 load_scale_rows(queues[item[2]], w2s_raw, 0, w2c_scales.rearrange("e s b n -> (e s) b n"))
+
+        for item in LOADS.split("|")[0].split():
+            load(item)
 
         def slot_list(first, count):
             return offsets[:, first // PER_COL : (first + count) // PER_COL]
@@ -174,7 +198,11 @@ def tile_moe_hot_s_mlp_silu_kernel(
                 for s in range(PASSES):
                     if e < HOT:
                         g = e * PASSES + s
-                        rhs, rhs_scale = w1[e][:, s, :].bitcast(FP8X4), w1hs[W1H_ROW:P, g * H : (g + 1) * H]
+                        rhs = w1[e][:, s, :].bitcast(FP8X4)
+                        if "hp" in LOADS:
+                            rhs_scale = (w1hs if g < 4 else w1hs2)[4 * (g % 4) : P, :]
+                        else:
+                            rhs_scale = w1hs[W1H_ROW:P, g * H : (g + 1) * H]
                     else:
                         g = (e - HOT) * PASSES + s
                         rhs, rhs_scale = w1[e][:, s, :].bitcast(FP4X4), w1cs[:, g * H : (g + 1) * H]
@@ -227,12 +255,13 @@ def tile_moe_hot_s_mlp_silu_kernel(
             )
 
         last = []
+        wide = {}
 
         def layer2(e):
             h_codes = held([P, C], U32, "h_codes%d" % e)
             h_scales = held([P, C], U8, "h_scales%d" % e)
             nc.vector.quantize_mx(out=h_codes[:].bitcast(FP8X4), scales=h_scales[:], in_=hq[e][:])
-            if e == E - 1:
+            if e == E - 1 and LAST != "n":
                 for j in range(C // BLK):
                     cols = slice(j * BLK, (j + 1) * BLK)
                     slots = slice(e * C + j * BLK, e * C + (j + 1) * BLK)
@@ -241,14 +270,25 @@ def tile_moe_hot_s_mlp_silu_kernel(
                     for t in range(4):
                         second_product(e, t, quarters[:, t, :], h_codes[:, cols], h_scales[:, cols])
                     half_q = held([P, 4 * BLK], BF16, "yq_last%d" % j)
-                    half = held([P, 4, BLK], F32, "y_last%d" % j)
+                    if j == 0:
+                        whole = held([P, 4, C], F32, "y_last")
+                    half = whole[:, :, cols] if LAST_WHOLE else held([P, 4, BLK], F32, "y_last%d" % j)
                     copies = {"v": nc.vector.tensor_copy, "s": nc.scalar.copy}
+                    if Y_FIRST:
+                        copies[LAST[2 * j + 1]](half[:], quarters)
                     copies[LAST[2 * j]](half_q[:].rearrange("p (s t) -> p s t", t=4), quarters.rearrange("p t s -> p s t"))
-                    copies[LAST[2 * j + 1]](half[:], quarters)
-                    nc.sync.dma_start(out=y_rows[:, :, slots], in_=half[:])
+                    if not Y_FIRST:
+                        copies[LAST[2 * j + 1]](half[:], quarters)
+                    if not LAST_WHOLE:
+                        nc.sync.dma_start(out=y_rows[:, :, slots], in_=half[:])
+                    elif j == 1:
+                        nc.sync.dma_start(out=y_rows[:, :, e * C : (e + 1) * C], in_=whole[:])
                     last.append((half_q, slots))
                 return
-            y[e] = held([P, 4, C], F32, "y%d" % e)
+            group = [gr for gr in Y_GROUPS + ((E - 1,),) if e in gr][0]
+            if e == group[0]:
+                wide[group] = held([P, 4, len(group) * C], F32, "y%d" % e)
+            y[e] = wide[group][:, :, (e - group[0]) * C : (e - group[0] + 1) * C]
             yq[e] = held([P, 4 * C], BF16, "yq%d" % e)
             if e in SCALAR_ROUNDS:
                 for j in range(C // BLK):
@@ -268,7 +308,14 @@ def tile_moe_hot_s_mlp_silu_kernel(
                         second_product(e, 2 * pair + v, acc[:, v * C : (v + 1) * C], h_codes[:], h_scales[:])
                     empty = nc.vector.tensor_copy if (e, pair) in VECTOR_EMPTIES else nc.scalar.copy
                     empty(y[e][:, 2 * pair : 2 * pair + 2, :], acc[:].rearrange("p (v s) -> p v s", v=2))
-            nc.sync.dma_start(out=y_rows[:, :, e * C : (e + 1) * C], in_=y[e][:])
+                    if e in BANK_STORES and len(group) == 1:
+                        nc.sync.dma_start(
+                            out=y_rows[:, 2 * pair : 2 * pair + 2, e * C : (e + 1) * C], in_=y[e][:, 2 * pair : 2 * pair + 2, :],
+                        )
+            if e in BANK_STORES and len(group) == 1 and e not in SCALAR_ROUNDS:
+                return
+            if e == group[-1]:
+                nc.sync.dma_start(out=y_rows[:, :, group[0] * C : (e + 1) * C], in_=wide[group][:])
 
         def round_y(e):
             if e not in SCALAR_ROUNDS:
@@ -278,21 +325,30 @@ def tile_moe_hot_s_mlp_silu_kernel(
 
         y_codes = held([P, SLOTS], I32, "y_codes")
 
+        stored = []
+
+        def store_scales(first, stop, names):
+            for q in range(4):
+                queues[names[q]].dma_start(
+                    out=out_2[0, 4 * q : 4 * q + 4, first:stop].bitcast(I32), in_=y_scales[32 * q : 32 * q + 4, first:stop].bitcast(I32),
+                )
+
         def planes(source, slots):
             nc.vector.quantize_mx(out=y_codes[:, slots].bitcast(FP8X4), scales=y_scales[:, slots], in_=source[:])
             if slots.stop in CODE_STORES:
                 first = max([0] + [c for c in CODE_STORES if c < slots.stop])
                 nc.sync.dma_start(out=word_rows[:, first : slots.stop], in_=y_codes[:, first : slots.stop])
+                stored.append(slots.stop)
+            if slots.stop == SCALE_SPLIT:
+                store_scales(0, SCALE_SPLIT, "yyyy")
 
         def rest_scales():
             for first, width in REST_CUTS:
                 gather_scales(sg_rest[:, first - FIRST * C : first - FIRST * C + width], first)
             cold0 = sg_rest[:, (HOT - FIRST) * C : (E - FIRST) * C]
-            if SHIFT == "g":
-                nc.gpsimd.dma_start(out=sg_cold1[0 : P - 4, :].bitcast(I32), in_=cold0[4:P, :].bitcast(I32))
-            else:
-                for r in range(4):
-                    queues[SHIFT].dma_start(out=sg_cold1[r:P:32, :].bitcast(I32), in_=cold0[4 + r : P : 32, :].bitcast(I32))
+            queues[SHIFT].dma_start(out=sg_cold1[0:112, :].bitcast(I32), in_=cold0[4:116, :].bitcast(I32))
+            for item in LOADS.split("|")[1].split():
+                load(item)
 
         for item in STEPS.split():
             e = int(item[1])
@@ -322,9 +378,10 @@ def tile_moe_hot_s_mlp_silu_kernel(
                 round_y(e)
             else:
                 planes(yq[e], slice(e * C, (e + 1) * C))
+        if LAST == "n":
+            round_y(E - 1)
+            planes(yq[E - 1], slice((E - 1) * C, E * C))
         for source, slots in last:
             planes(source, slots)
-        for q in range(4):
-            queues[SCALE_STORES[q]].dma_start(
-                out=out_2[0, 4 * q : 4 * q + 4, :].bitcast(I32), in_=y_scales[32 * q : 32 * q + 4, :].bitcast(I32),
-            )
+        assert stored == sorted(CODE_STORES)
+        store_scales(SCALE_SPLIT, SLOTS, SCALE_STORES)

@@ -25,26 +25,31 @@ PER_COL = 16
 W1H_ROW = 4
 W2H_ROW = 8
 SCALAR_ROUNDS = ()
-VECTOR_TURNED = (3,4)
-VECTOR_EMPTIES = ()
-LOADS = "x0 x1 xs a0 hay a1 a2 cag a3 b0 hby | cbg b1 a4 a5 b2 b3"
+VECTOR_TURNED = (4,5)
+VECTOR_EMPTIES = ((1,1),(5,1))
+LOADS = "x0 x1 xs a0 hay a1 b0 hby cbg a2 cag a3 | b1 a4 b2 a5 b3"
 FIRST = 2
 GATE = "x"
 REST_CUTS = ((1024, 512), (512, 512))
 XG_BUFS = (2,2)
-BANKS = (3,1,4)
+BANKS = (3,2,3)
 SHIFT = "y"
-CODE_STORES = (256,768,1280,1536)
+CODE_STORES = (512,1024,1408,1536)
 SCALE_STORES = "ssss"
-STEPS = "g0 s0 g1 g2 s1 g3 s2 A0 d0 d4 d1 g4 d3 e1 d2 e0 e2 B0 A1 A2 B1 A3 r0 r1 p0 g5 p1 A4 B2 B3 r2 B4 A5 d5 r4 r3 p2 p3 p4 B5"
-LAST = "n"
+STEPS = "g0 s0 g1 s1 s2 d4 g2 A0 d0 e0 g3 B0 d3 d1 A1 e2 A2 d5 g4 e1 g5 A3 d2 A4 r0 B1 A5 B2 r2 p0 r1 B3 r3 B4 p1 p2 p3 r4 p4 B5"
+LAST = "vsss"
 REUSE = {}
 Y_GROUPS = ((0,),(1,),(2,),(3,),(4,))
-LAST_WHOLE = False
+LAST_WHOLE = True
 Y_FIRST = True
-BANK_STORES = (3,4,5)
+BANK_STORES = (0,1,2,3,4,5)
 SCALE_SPLIT = 0
-XS_QUEUES = "ggyy"
+XS_QUEUES = "yyyy"
+GATHER_GROUPS = ((0,),(1,),(2,3),(4,),(5,))
+MERGE_FIRST = False
+DEAL_GROUPS = ((0,1),(2,),(3,4,5))
+SCALE_GROUPS = ((0,1,2),)
+PACK = True
 
 
 def load_scale_rows(queue, plane, row0, rows):
@@ -78,7 +83,10 @@ def tile_moe_hot_s_mlp_silu_kernel(
             w1hs = held([P, HOT * PASSES * H], U8, "w1hs")
             late_planes = ()
         w1cs = held([P, COLD * PASSES * H], U8, "w1cs")
-        w2s_raw = held([P, HOT * N], U8, "w2s_raw")
+        w2s_raw = held([P, N if PACK else HOT * N], U8, "w2s_raw")
+        if PACK:
+            w2cs = held([P, COLD * N], U8, "w2cs")
+            late_planes = late_planes + (w2cs,)
         sg_cold1 = held([P, COLD * C], U8, "sg_cold1")
         ident = held([P, P], F32, "ident")
 
@@ -100,6 +108,7 @@ def tile_moe_hot_s_mlp_silu_kernel(
 
         w1 = [None] * E
         w2_raw = [None] * E
+        w2h_raw = held([P, HOT * N], I32, "w2h_raw")
 
         def load_w1(e):
             if e < HOT:
@@ -111,7 +120,7 @@ def tile_moe_hot_s_mlp_silu_kernel(
 
         def load_w2(e):
             if e < HOT:
-                w2_raw[e] = held([P, N], I32, "w2h_raw%d" % e)
+                w2_raw[e] = w2h_raw[:, e * N : (e + 1) * N]
                 nc.sync.dma_start(out=w2_raw[e][:], in_=w2h_words[e, 0].rearrange("p n d -> p (n d)").bitcast(I32))
             else:
                 w2_raw[e] = held([P, COLD * N // 2], I32, "w2c_raw")
@@ -132,7 +141,7 @@ def tile_moe_hot_s_mlp_silu_kernel(
                 for f in range(COLD):
                     w1[HOT + f] = cold[:, f * PASSES : (f + 1) * PASSES, :]
             elif item == "B":
-                hot = held([P, HOT * N], I32, "w2h_raw")
+                hot = w2h_raw
                 nc.sync.dma_start(
                     out=hot[:].rearrange("p (e w) -> p e w", e=HOT), in_=w2h_words.rearrange("e s p n d -> p (e s) (n d)").bitcast(I32),
                 )
@@ -153,6 +162,12 @@ def tile_moe_hot_s_mlp_silu_kernel(
                 load_scale_rows(queues[item[2]], w1hs, W1H_ROW, w1h_scales.rearrange("e s b i -> (e s) b i"))
             elif item.startswith("ca"):
                 load_scale_rows(queues[item[2]], w1cs, 0, w1c_scales.rearrange("e s b i -> (e s) b i"))
+            elif PACK and item[1] == "b":
+                rows, row0 = (w2h_scales, 4) if item[0] == "h" else (w2c_scales, 16)
+                for q in range(4):
+                    queues[item[2]].dma_start(
+                        out=w2s_raw[32 * q + row0 : 32 * q + row0 + 12, :].bitcast(I32), in_=rows[:, 0, 4 * q : 4 * q + 4, :].bitcast(I32),
+                    )
             elif item.startswith("hb"):
                 load_scale_rows(queues[item[2]], w2s_raw, W2H_ROW, w2h_scales.rearrange("e s b n -> (e s) b n"))
             else:
@@ -164,19 +179,26 @@ def tile_moe_hot_s_mlp_silu_kernel(
         def slot_list(first, count):
             return offsets[:, first // PER_COL : (first + count) // PER_COL]
 
-        sg_own = [keep.tile([P, C], U8, name="sg_own%d" % e, tag="sg%d" % e, align_bytes=64) for e in range(FIRST)]
+        sg_first = held([P, FIRST * C], U8, "sg_first")
+        sg_own = [sg_first[:, e * C : (e + 1) * C] for e in range(FIRST)]
         sg_rest = keep.tile([P, (E - FIRST) * C], U8, name="sg_rest", tag="sg%s" % GATE, align_bytes=64)
         xg = [[None] * PASSES for e in range(E)]
 
         def gather_words(e):
+            group = [gr for gr in GATHER_GROUPS if e in gr][0]
+            if e != group[0]:
+                return
+            width = len(group) * C
             if e in REUSE:
-                both = keep.tile([P, PASSES * C], U32, name="xg_both%d" % e, tag="w1h%d" % REUSE[e], align_bytes=64)
+                both = keep.tile([P, PASSES * width], U32, name="xg_both%d" % e, tag="w1h%d" % REUSE[e], align_bytes=64)
             for s in range(PASSES):
                 if e in REUSE:
-                    xg[e][s] = both[:, s * C : (s + 1) * C]
+                    dst = both[:, s * width : (s + 1) * width]
                 else:
-                    xg[e][s] = ring.tile([P, C], U32, name="xg%d" % s, bufs=XG_BUFS[s], align_bytes=64)
-                nc.vector.tensor_copy(xg[e][s][:], xw[s][:].bitcast(U32).indirect(slot_list(e * C, C)))
+                    dst = ring.tile([P, width], U32, name="xg%d" % s, bufs=XG_BUFS[s], align_bytes=64)
+                nc.vector.tensor_copy(dst[:], xw[s][:].bitcast(U32).indirect(slot_list(e * C, width)))
+                for n, other in enumerate(group):
+                    xg[other][s] = dst[:, n * C : (n + 1) * C]
 
         def gather_scales(dst, first):
             nc.vector.tensor_copy(dst, xs[:].indirect(slot_list(first, dst.shape[1])))
@@ -220,7 +242,7 @@ def tile_moe_hot_s_mlp_silu_kernel(
             empty = nc.vector.tensor_copy if e in VECTOR_TURNED else nc.scalar.copy
             empty(hq[e][:].bitcast(F32).rearrange("p (j s u) -> p j s u", j=2, u=2), turned[:].rearrange("p j u s -> p j s u"))
 
-        w2s = [held([P, N], U8, "w2s%d" % f) for f in range(HOT)]
+        w2s_all = held([P, N if PACK else HOT * N], U8, "w2s")
         y_scales = held([P, SLOTS], U8, "y_scales")
         y_rows = out_0.rearrange("(p t) j -> p t j", t=4)
         word_rows = out_1[0].rearrange("p j d -> p (j d)").bitcast(I32)
@@ -228,28 +250,53 @@ def tile_moe_hot_s_mlp_silu_kernel(
         y = [None] * E
         yq = [None] * E
 
-        def deal(dst, src, width):
-            line = 16 * dst.shape[1] // width
+        def deal(dst, src, line):
+            count = dst.shape[1] // N
             nc.vector.tensor_copy(
-                dst.rearrange("p (t b i) -> p b t i", t=4, i=line), src.rearrange("p (b i t) -> p b t i", t=4, i=line),
+                dst.rearrange("p (f t b i) -> p b f t i", f=count, t=4, i=line),
+                src.rearrange("p (f b i t) -> p b f t i", f=count, t=4, i=line),
             )
 
+        w2h = held([P, HOT * N], I32, "w2h")
+        w2c = held([P, COLD * N // 2], I32, "w2c")
+
         def deal_w2(e):
+            group = [gr for gr in DEAL_GROUPS if e in gr][0]
+            first, stop = group[0], group[-1] + 1
             if e < HOT:
-                w2[e] = held([P, N], I32, "w2h%d" % e)
-                deal(w2[e][:], w2_raw[e][:], 4 * N)
+                w2[e] = w2h[:, e * N : (e + 1) * N]
+                if e == first:
+                    deal(w2h[:, first * N : stop * N], w2h_raw[:, first * N : stop * N], 4)
             else:
-                f = e - HOT
-                w2[e] = held([P, N // 2], I32, "w2c%d" % f)
-                deal(w2[e][:].bitcast(U16), w2_raw[HOT][:, f * N // 2 : (f + 1) * N // 2].bitcast(U16), 2 * N)
+                w2[e] = w2c[:, (e - HOT) * N // 2 : (e - HOT + 1) * N // 2]
+                if e == first:
+                    cols = slice((first - HOT) * N // 2, (stop - HOT) * N // 2)
+                    deal(w2c[:, cols].bitcast(U16), w2_raw[HOT][:, cols].bitcast(U16), 8)
+
+        def deal_scales(f):
+            if PACK:
+                if f == 0:
+                    deal(w2s_all[:], w2s_raw[:], 16)
+                    for c in range(COLD):
+                        nc.sync.dma_start(
+                            out=w2cs[0:100, c * N : (c + 1) * N].bitcast(I32), in_=w2s_all[16 + 4 * c : 116 + 4 * c, :].bitcast(I32),
+                        )
+                return
+            group = [gr for gr in SCALE_GROUPS if f in gr][0]
+            if f == group[0]:
+                cols = slice(f * N, (group[-1] + 1) * N)
+                deal(w2s_all[:, cols], w2s_raw[:, cols], 16)
 
         def second_product(e, t, out, codes, scales):
             if e < HOT:
                 lhsT = w2[e][:, t * P : (t + 1) * P].bitcast(FP8X4)
-                lhsT_scale = w2s[e][W2H_ROW:P, t * P : (t + 1) * P]
+                if PACK:
+                    lhsT_scale = w2s_all[4 + 4 * e : P, t * P : (t + 1) * P]
+                else:
+                    lhsT_scale = w2s_all[W2H_ROW:P, e * N + t * P : e * N + (t + 1) * P]
             else:
                 lhsT = w2[e][:, t * P // 2 : (t + 1) * P // 2].bitcast(FP4X4)
-                lhsT_scale = w2s[e - HOT][:, t * P : (t + 1) * P]
+                lhsT_scale = (w2cs if PACK else w2s_all)[:, (e - HOT) * N + t * P : (e - HOT) * N + (t + 1) * P]
             nc.tensor.matmul_mx(
                 out=out, lhsT=lhsT, lhsT_scale=lhsT_scale, rhs=codes.bitcast(FP8X4), rhs_scale=scales, start=True, stop=True,
             )
@@ -320,7 +367,7 @@ def tile_moe_hot_s_mlp_silu_kernel(
         def round_y(e):
             if e not in SCALAR_ROUNDS:
                 nc.vector.tensor_copy(
-                    yq[e][:].rearrange("p (c i t) -> p c t i", i=4, t=4), y[e][:].rearrange("p t (c i) -> p c t i", i=4),
+                    yq[e][:].rearrange("p (c i t) -> p c t i", i=2, t=4), y[e][:].rearrange("p t (c i) -> p c t i", i=2),
                 )
 
         y_codes = held([P, SLOTS], I32, "y_codes")
@@ -354,7 +401,10 @@ def tile_moe_hot_s_mlp_silu_kernel(
             e = int(item[1])
             if item[0] == "s":
                 if e < FIRST:
-                    gather_scales(sg_own[e][:], e * C)
+                    if not MERGE_FIRST:
+                        gather_scales(sg_own[e], e * C)
+                    elif e == 0:
+                        gather_scales(sg_first[:], 0)
                 else:
                     rest_scales()
             elif item[0] == "w":
@@ -369,7 +419,7 @@ def tile_moe_hot_s_mlp_silu_kernel(
             elif item[0] == "A":
                 layer1(e)
             elif item[0] == "e":
-                deal(w2s[e][:], w2s_raw[:, e * N : (e + 1) * N], N)
+                deal_scales(e)
             elif item[0] == "d":
                 deal_w2(e)
             elif item[0] == "B":

from contextlib import ExitStack

import concourse.mybir as mybir
from concourse.masks import make_identity

K, T, E, C, H, N, HOT = 1024, 768, 6, 256, 512, 512, 3
COLD = E - HOT
SLOTS = E * C
FLOPS = 2 * SLOTS * (K * H + H * N)

F32 = mybir.dt.float32
BF16 = mybir.dt.bfloat16
I32 = mybir.dt.int32
U32 = mybir.dt.uint32
U16 = mybir.dt.uint16
U8 = mybir.dt.uint8
FP8X4 = mybir.dt.float8_e4m3fn_x4
FP4X4 = mybir.dt.float4_e2m1fn_x4
SILU = mybir.ActivationFunctionType.Silu

P = 128
PASSES = K // 512
BLK = 128
PER_COL = 16
W1H_ROW = 4
W2H_ROW = 8
SCALAR_ROUNDS = ()
VECTOR_TURNED = (4,5)
VECTOR_EMPTIES = ((1,1),(5,1))
LOADS = "x0 x1 xs a0 hay a1 b0 hby cbg a2 cag a3 | b1 a4 b2 a5 b3"
FIRST = 2
GATE = "x"
REST_CUTS = ((1024, 512), (512, 512))
XG_BUFS = (2,2)
BANKS = (3,2,3)
SHIFT = "y"
CODE_STORES = (512,1024,1408,1536)
SCALE_STORES = "ssss"
STEPS = "g0 s0 g1 s1 s2 d4 g2 A0 d0 e0 g3 B0 d3 d1 A1 e2 A2 d5 g4 e1 g5 A3 d2 A4 r0 B1 A5 B2 r2 p0 r1 B3 r3 B4 p1 p2 p3 r4 p4 B5"
LAST = "vsss"
REUSE = {}
Y_GROUPS = ((0,),(1,),(2,),(3,),(4,))
LAST_WHOLE = True
Y_FIRST = True
BANK_STORES = (0,1,2,3,4,5)
SCALE_SPLIT = 0
XS_QUEUES = "yyyy"
GATHER_GROUPS = ((0,),(1,),(2,3),(4,),(5,))
MERGE_FIRST = False
DEAL_GROUPS = ((0,1),(2,),(3,4,5))
SCALE_GROUPS = ((0,1,2),)
PACK = True


def load_scale_rows(queue, plane, row0, rows):
    planes = rows.shape[0]
    by_r = rows.rearrange("g (q r) j -> r q g j", r=4)
    for r in range(4):
        dst = plane[row0 + r : P : 32, :].bitcast(I32).rearrange("q (g j) -> q g j", g=planes)
        queue.dma_start(out=dst, in_=by_r[r].bitcast(I32))


def tile_moe_hot_s_mlp_silu_kernel(
    tc, x_words, x_scales, w1h_words, w1h_scales, w2h_words, w2h_scales,
    w1c_words, w1c_scales, w2c_words, w2c_scales, offs, out_0, out_1, out_2,
):
    nc = tc.nc
    with ExitStack() as ctx:
        keep = ctx.enter_context(tc.tile_pool(name="keep", bufs=1))
        ring = ctx.enter_context(tc.tile_pool(name="ring", bufs=4))
        psum = ctx.enter_context(tc.psum_pool(name="psum", bufs=1))

        def held(shape, dtype, name):
            return keep.tile(shape, dtype, name=name, align_bytes=64)

        offsets = keep.tile([P, SLOTS // PER_COL], U16, name="offsets")
        xs = held([P, T], U8, "xs")
        if "hp" in LOADS:
            w1hs = held([P, H], U8, "w1hs")
            w1hs2 = held([P, H], U8, "w1hs2")
            late_planes = (w1hs2,)
        else:
            w1hs = held([P, HOT * PASSES * H], U8, "w1hs")
            late_planes = ()
        w1cs = held([P, COLD * PASSES * H], U8, "w1cs")
        w2s_raw = held([P, N if PACK else HOT * N], U8, "w2s_raw")
        if PACK:
            w2cs = held([P, COLD * N], U8, "w2cs")
            late_planes = late_planes + (w2cs,)
        sg_cold1 = held([P, COLD * C], U8, "sg_cold1")
        ident = held([P, P], F32, "ident")

        for plane in (xs, w1hs, w2s_raw, w1cs, sg_cold1) + late_planes:
            nc.vector.memset(plane[:].bitcast(I32), 0)

        nc.sync.dma_start(offsets[:], offs)
        xw = [held([P, T], I32, "xw%d" % s) for s in range(PASSES)]

        def load_x(s):
            nc.sync.dma_start(out=xw[s][:], in_=x_words[s].rearrange("p t d -> p (t d)").bitcast(I32))

        def load_xs():
            for q in range(4):
                queues[XS_QUEUES[q]].dma_start(
                    out=xs[32 * q : 32 * q + 8, :].bitcast(I32), in_=x_scales[:, 4 * q : 4 * q + 4, :].bitcast(I32),
                )
            make_identity(nc, ident[:])

        w1 = [None] * E
        w2_raw = [None] * E
        w2h_raw = held([P, HOT * N], I32, "w2h_raw")

        def load_w1(e):
            if e < HOT:
                w1[e] = keep.tile([P, PASSES, H], I32, name="w1h%d" % e, tag="w1h%d" % e, align_bytes=64)
                nc.sync.dma_start(out=w1[e][:], in_=w1h_words[e].rearrange("s p i d -> p s (i d)").bitcast(I32))
            else:
                w1[e] = held([P, PASSES, H // 2], I32, "w1c%d" % e)
                nc.sync.dma_start(out=w1[e][:], in_=w1c_words[e - HOT].rearrange("s p b -> p s b").bitcast(I32))

        def load_w2(e):
            if e < HOT:
                w2_raw[e] = w2h_raw[:, e * N : (e + 1) * N]
                nc.sync.dma_start(out=w2_raw[e][:], in_=w2h_words[e, 0].rearrange("p n d -> p (n d)").bitcast(I32))
            else:
                w2_raw[e] = held([P, COLD * N // 2], I32, "w2c_raw")
                nc.sync.dma_start(
                    out=w2_raw[e][:].rearrange("p (f b) -> p f b", f=COLD),
                    in_=w2c_words.rearrange("f s p b -> p (f s) b").bitcast(I32),
                )

        queues = {"y": nc.sync, "s": nc.scalar, "g": nc.gpsimd}
        def load(item):
            if item == "xs":
                load_xs()
            elif item.startswith("x"):
                load_x(int(item[1]))
            elif item == "C":
                cold = held([P, COLD * PASSES, H // 2], I32, "w1c")
                nc.sync.dma_start(out=cold[:], in_=w1c_words.rearrange("f s p b -> p (f s) b").bitcast(I32))
                for f in range(COLD):
                    w1[HOT + f] = cold[:, f * PASSES : (f + 1) * PASSES, :]
            elif item == "B":
                hot = w2h_raw
                nc.sync.dma_start(
                    out=hot[:].rearrange("p (e w) -> p e w", e=HOT), in_=w2h_words.rearrange("e s p n d -> p (e s) (n d)").bitcast(I32),
                )
                for e in range(HOT):
                    w2_raw[e] = hot[:, e * N : (e + 1) * N]
            elif item.startswith("a"):
                load_w1(int(item[1]))
            elif item.startswith("b"):
                load_w2(int(item[1]))
            elif item.startswith("hp") or item.startswith("hq"):
                rows = w1h_scales.rearrange("e s b i -> (e s) b i")
                plane, rows = (w1hs, rows[0:4]) if item[1] == "p" else (w1hs2, rows[4:6])
                for q in range(4):
                    queues[item[2]].dma_start(
                        out=plane[32 * q : 32 * q + 4 * rows.shape[0], :].bitcast(I32), in_=rows[:, 4 * q : 4 * q + 4, :].bitcast(I32),
                    )
            elif item.startswith("ha"):
                load_scale_rows(queues[item[2]], w1hs, W1H_ROW, w1h_scales.rearrange("e s b i -> (e s) b i"))
            elif item.startswith("ca"):
                load_scale_rows(queues[item[2]], w1cs, 0, w1c_scales.rearrange("e s b i -> (e s) b i"))
            elif PACK and item[1] == "b":
                rows, row0 = (w2h_scales, 4) if item[0] == "h" else (w2c_scales, 16)
                for q in range(4):
                    queues[item[2]].dma_start(
                        out=w2s_raw[32 * q + row0 : 32 * q + row0 + 12, :].bitcast(I32), in_=rows[:, 0, 4 * q : 4 * q + 4, :].bitcast(I32),
                    )
            elif item.startswith("hb"):
                load_scale_rows(queues[item[2]], w2s_raw, W2H_ROW, w2h_scales.rearrange("e s b n -> (e s) b n"))
            else:
                load_scale_rows(queues[item[2]], w2s_raw, 0, w2c_scales.rearrange("e s b n -> (e s) b n"))

        for item in LOADS.split("|")[0].split():
            load(item)

        def slot_list(first, count):
            return offsets[:, first // PER_COL : (first + count) // PER_COL]

        sg_first = held([P, FIRST * C], U8, "sg_first")
        sg_own = [sg_first[:, e * C : (e + 1) * C] for e in range(FIRST)]
        sg_rest = keep.tile([P, (E - FIRST) * C], U8, name="sg_rest", tag="sg%s" % GATE, align_bytes=64)
        xg = [[None] * PASSES for e in range(E)]

        def gather_words(e):
            group = [gr for gr in GATHER_GROUPS if e in gr][0]
            if e != group[0]:
                return
            width = len(group) * C
            if e in REUSE:
                both = keep.tile([P, PASSES * width], U32, name="xg_both%d" % e, tag="w1h%d" % REUSE[e], align_bytes=64)
            for s in range(PASSES):
                if e in REUSE:
                    dst = both[:, s * width : (s + 1) * width]
                else:
                    dst = ring.tile([P, width], U32, name="xg%d" % s, bufs=XG_BUFS[s], align_bytes=64)
                nc.vector.tensor_copy(dst[:], xw[s][:].bitcast(U32).indirect(slot_list(e * C, width)))
                for n, other in enumerate(group):
                    xg[other][s] = dst[:, n * C : (n + 1) * C]

        def gather_scales(dst, first):
            nc.vector.tensor_copy(dst, xs[:].indirect(slot_list(first, dst.shape[1])))

        def token_scales(e, s, j):
            if e < FIRST:
                return sg_own[e][4 * s : P, j * BLK : (j + 1) * BLK]
            if e < HOT or s == 0:
                return sg_rest[4 * s : P, (e - FIRST) * C + j * BLK : (e - FIRST) * C + (j + 1) * BLK]
            first = (e - HOT) * C + j * BLK
            return sg_cold1[:, first : first + BLK]

        hq = [held([P, 4 * C], BF16, "hq%d" % e) for e in range(E)]

        def layer1(e):
            turned = psum.tile([P, 2, 2, BLK], F32, name="turned", bufs=BANKS[1])
            for j in range(C // BLK):
                acc = psum.tile([P, H], F32, name="acc1", bufs=BANKS[0])
                for s in range(PASSES):
                    if e < HOT:
                        g = e * PASSES + s
                        rhs = w1[e][:, s, :].bitcast(FP8X4)
                        if "hp" in LOADS:
                            rhs_scale = (w1hs if g < 4 else w1hs2)[4 * (g % 4) : P, :]
                        else:
                            rhs_scale = w1hs[W1H_ROW:P, g * H : (g + 1) * H]
                    else:
                        g = (e - HOT) * PASSES + s
                        rhs, rhs_scale = w1[e][:, s, :].bitcast(FP4X4), w1cs[:, g * H : (g + 1) * H]
                    nc.tensor.matmul_mx(
                        out=acc[:], lhsT=xg[e][s][:, j * BLK : (j + 1) * BLK].bitcast(FP8X4), lhsT_scale=token_scales(e, s, j),
                        rhs=rhs, rhs_scale=rhs_scale, start=(s == 0), stop=(s == PASSES - 1),
                    )
                hs = ring.tile([P, H], BF16, name="hs", align_bytes=64)
                nc.scalar.activation(
                    hs[:].rearrange("p (u q v) -> p u q v", u=2, v=2), acc[:].rearrange("p (q u v) -> p u q v", u=2, v=2), SILU,
                )
                words = hs[:].bitcast(F32)
                for u in range(2):
                    nc.tensor.transpose(turned[:, j, u, :], words[:, u * P : (u + 1) * P], ident[:])
            empty = nc.vector.tensor_copy if e in VECTOR_TURNED else nc.scalar.copy
            empty(hq[e][:].bitcast(F32).rearrange("p (j s u) -> p j s u", j=2, u=2), turned[:].rearrange("p j u s -> p j s u"))

        w2s_all = held([P, N if PACK else HOT * N], U8, "w2s")
        y_scales = held([P, SLOTS], U8, "y_scales")
        y_rows = out_0.rearrange("(p t) j -> p t j", t=4)
        word_rows = out_1[0].rearrange("p j d -> p (j d)").bitcast(I32)
        w2 = [None] * E
        y = [None] * E
        yq = [None] * E

        def deal(dst, src, line):
            count = dst.shape[1] // N
            nc.vector.tensor_copy(
                dst.rearrange("p (f t b i) -> p b f t i", f=count, t=4, i=line),
                src.rearrange("p (f b i t) -> p b f t i", f=count, t=4, i=line),
            )

        w2h = held([P, HOT * N], I32, "w2h")
        w2c = held([P, COLD * N // 2], I32, "w2c")

        def deal_w2(e):
            group = [gr for gr in DEAL_GROUPS if e in gr][0]
            first, stop = group[0], group[-1] + 1
            if e < HOT:
                w2[e] = w2h[:, e * N : (e + 1) * N]
                if e == first:
                    deal(w2h[:, first * N : stop * N], w2h_raw[:, first * N : stop * N], 4)
            else:
                w2[e] = w2c[:, (e - HOT) * N // 2 : (e - HOT + 1) * N // 2]
                if e == first:
                    cols = slice((first - HOT) * N // 2, (stop - HOT) * N // 2)
                    deal(w2c[:, cols].bitcast(U16), w2_raw[HOT][:, cols].bitcast(U16), 8)

        def deal_scales(f):
            if PACK:
                if f == 0:
                    deal(w2s_all[:], w2s_raw[:], 16)
                    for c in range(COLD):
                        nc.sync.dma_start(
                            out=w2cs[0:100, c * N : (c + 1) * N].bitcast(I32), in_=w2s_all[16 + 4 * c : 116 + 4 * c, :].bitcast(I32),
                        )
                return
            group = [gr for gr in SCALE_GROUPS if f in gr][0]
            if f == group[0]:
                cols = slice(f * N, (group[-1] + 1) * N)
                deal(w2s_all[:, cols], w2s_raw[:, cols], 16)

        def second_product(e, t, out, codes, scales):
            if e < HOT:
                lhsT = w2[e][:, t * P : (t + 1) * P].bitcast(FP8X4)
                if PACK:
                    lhsT_scale = w2s_all[4 + 4 * e : P, t * P : (t + 1) * P]
                else:
                    lhsT_scale = w2s_all[W2H_ROW:P, e * N + t * P : e * N + (t + 1) * P]
            else:
                lhsT = w2[e][:, t * P // 2 : (t + 1) * P // 2].bitcast(FP4X4)
                lhsT_scale = (w2cs if PACK else w2s_all)[:, (e - HOT) * N + t * P : (e - HOT) * N + (t + 1) * P]
            nc.tensor.matmul_mx(
                out=out, lhsT=lhsT, lhsT_scale=lhsT_scale, rhs=codes.bitcast(FP8X4), rhs_scale=scales, start=True, stop=True,
            )

        last = []
        wide = {}

        def layer2(e):
            h_codes = held([P, C], U32, "h_codes%d" % e)
            h_scales = held([P, C], U8, "h_scales%d" % e)
            nc.vector.quantize_mx(out=h_codes[:].bitcast(FP8X4), scales=h_scales[:], in_=hq[e][:])
            if e == E - 1 and LAST != "n":
                for j in range(C // BLK):
                    cols = slice(j * BLK, (j + 1) * BLK)
                    slots = slice(e * C + j * BLK, e * C + (j + 1) * BLK)
                    acc = psum.tile([P, 4 * BLK], F32, name="acc2", bufs=BANKS[2])
                    quarters = acc[:].rearrange("p (t s) -> p t s", t=4)
                    for t in range(4):
                        second_product(e, t, quarters[:, t, :], h_codes[:, cols], h_scales[:, cols])
                    half_q = held([P, 4 * BLK], BF16, "yq_last%d" % j)
                    if j == 0:
                        whole = held([P, 4, C], F32, "y_last")
                    half = whole[:, :, cols] if LAST_WHOLE else held([P, 4, BLK], F32, "y_last%d" % j)
                    copies = {"v": nc.vector.tensor_copy, "s": nc.scalar.copy}
                    if Y_FIRST:
                        copies[LAST[2 * j + 1]](half[:], quarters)
                    copies[LAST[2 * j]](half_q[:].rearrange("p (s t) -> p s t", t=4), quarters.rearrange("p t s -> p s t"))
                    if not Y_FIRST:
                        copies[LAST[2 * j + 1]](half[:], quarters)
                    if not LAST_WHOLE:
                        nc.sync.dma_start(out=y_rows[:, :, slots], in_=half[:])
                    elif j == 1:
                        nc.sync.dma_start(out=y_rows[:, :, e * C : (e + 1) * C], in_=whole[:])
                    last.append((half_q, slots))
                return
            group = [gr for gr in Y_GROUPS + ((E - 1,),) if e in gr][0]
            if e == group[0]:
                wide[group] = held([P, 4, len(group) * C], F32, "y%d" % e)
            y[e] = wide[group][:, :, (e - group[0]) * C : (e - group[0] + 1) * C]
            yq[e] = held([P, 4 * C], BF16, "yq%d" % e)
            if e in SCALAR_ROUNDS:
                for j in range(C // BLK):
                    cols = slice(j * BLK, (j + 1) * BLK)
                    acc = psum.tile([P, 4 * BLK], F32, name="acc2", bufs=BANKS[2])
                    quarters = acc[:].rearrange("p (t s) -> p t s", t=4)
                    for t in range(4):
                        second_product(e, t, quarters[:, t, :], h_codes[:, cols], h_scales[:, cols])
                    nc.scalar.copy(y[e][:, :, cols], quarters)
                    nc.scalar.copy(
                        yq[e][:, 4 * j * BLK : 4 * (j + 1) * BLK].rearrange("p (s t) -> p s t", t=4), quarters.rearrange("p t s -> p s t"),
                    )
            else:
                for pair in range(2):
                    acc = psum.tile([P, 2 * C], F32, name="acc2", bufs=BANKS[2])
                    for v in range(2):
                        second_product(e, 2 * pair + v, acc[:, v * C : (v + 1) * C], h_codes[:], h_scales[:])
                    empty = nc.vector.tensor_copy if (e, pair) in VECTOR_EMPTIES else nc.scalar.copy
                    empty(y[e][:, 2 * pair : 2 * pair + 2, :], acc[:].rearrange("p (v s) -> p v s", v=2))
                    if e in BANK_STORES and len(group) == 1:
                        nc.sync.dma_start(
                            out=y_rows[:, 2 * pair : 2 * pair + 2, e * C : (e + 1) * C], in_=y[e][:, 2 * pair : 2 * pair + 2, :],
                        )
            if e in BANK_STORES and len(group) == 1 and e not in SCALAR_ROUNDS:
                return
            if e == group[-1]:
                nc.sync.dma_start(out=y_rows[:, :, group[0] * C : (e + 1) * C], in_=wide[group][:])

        def round_y(e):
            if e not in SCALAR_ROUNDS:
                nc.vector.tensor_copy(
                    yq[e][:].rearrange("p (c i t) -> p c t i", i=2, t=4), y[e][:].rearrange("p t (c i) -> p c t i", i=2),
                )

        y_codes = held([P, SLOTS], I32, "y_codes")

        stored = []

        def store_scales(first, stop, names):
            for q in range(4):
                queues[names[q]].dma_start(
                    out=out_2[0, 4 * q : 4 * q + 4, first:stop].bitcast(I32), in_=y_scales[32 * q : 32 * q + 4, first:stop].bitcast(I32),
                )

        def planes(source, slots):
            nc.vector.quantize_mx(out=y_codes[:, slots].bitcast(FP8X4), scales=y_scales[:, slots], in_=source[:])
            if slots.stop in CODE_STORES:
                first = max([0] + [c for c in CODE_STORES if c < slots.stop])
                nc.sync.dma_start(out=word_rows[:, first : slots.stop], in_=y_codes[:, first : slots.stop])
                stored.append(slots.stop)
            if slots.stop == SCALE_SPLIT:
                store_scales(0, SCALE_SPLIT, "yyyy")

        def rest_scales():
            for first, width in REST_CUTS:
                gather_scales(sg_rest[:, first - FIRST * C : first - FIRST * C + width], first)
            cold0 = sg_rest[:, (HOT - FIRST) * C : (E - FIRST) * C]
            queues[SHIFT].dma_start(out=sg_cold1[0:112, :].bitcast(I32), in_=cold0[4:116, :].bitcast(I32))
            for item in LOADS.split("|")[1].split():
                load(item)

        for item in STEPS.split():
            e = int(item[1])
            if item[0] == "s":
                if e < FIRST:
                    if not MERGE_FIRST:
                        gather_scales(sg_own[e], e * C)
                    elif e == 0:
                        gather_scales(sg_first[:], 0)
                else:
                    rest_scales()
            elif item[0] == "w":
                idle = psum.tile([P, H], F32, name="acc2", bufs=BANKS[2])
                for n in range(e):
                    nc.tensor.matmul_mx(
                        out=idle[:, (n % 2) * C : (n % 2 + 1) * C], lhsT=xg[0][0][:, 0:BLK].bitcast(FP8X4), lhsT_scale=sg_own[0][:, 0:BLK],
                        rhs=xg[0][0][:].bitcast(FP8X4), rhs_scale=sg_own[0][:], start=True, stop=True,
                    )
            elif item[0] == "g":
                gather_words(e)
            elif item[0] == "A":
                layer1(e)
            elif item[0] == "e":
                deal_scales(e)
            elif item[0] == "d":
                deal_w2(e)
            elif item[0] == "B":
                layer2(e)
            elif item[0] == "r":
                round_y(e)
            else:
                planes(yq[e], slice(e * C, (e + 1) * C))
        if LAST == "n":
            round_y(E - 1)
            planes(yq[E - 1], slice((E - 1) * C, E * C))
        for source, slots in last:
            planes(source, slots)
        assert stored == sorted(CODE_STORES)
        store_scales(SCALE_SPLIT, SLOTS, SCALE_STORES)
